import numpy as np
import ml_dtypes


def mxq(x, axis, fmt="e4m3"):
    dtype, down = {"e4m3": (ml_dtypes.float8_e4m3fn, 7), "e5m2": (ml_dtypes.float8_e5m2, 14)}[fmt]
    v = np.moveaxis(np.asarray(x, np.float32).astype(ml_dtypes.bfloat16).astype(np.float64), axis, -1)
    blocks = v.reshape(v.shape[:-1] + (-1, 32))
    amax = np.abs(blocks).max(-1, keepdims=True)
    byte = np.maximum(np.where(amax > 0, np.frexp(amax)[1] - 1 + 127, 0) - down, 1)
    scale = np.exp2(byte - 127.0)
    codes = (blocks / scale).astype(np.float32).astype(dtype).astype(np.float64)
    return np.moveaxis((codes * scale).reshape(v.shape), -1, axis)


WIDE = False


def mx_kscale(k):
    if not WIDE:
        return np.ones(k)
    levels = np.array([10, -10, 5, -5, 0])
    if k % 512:
        return np.exp2(np.random.permutation(np.resize(levels, k // 32))).repeat(32)
    a = np.empty((k // 512, 16))
    for p in range(k // 512):
        a[p, :8] = np.random.permutation(np.resize(levels, 8))
        for g in range(8):
            far = levels[np.abs(levels - a[p, g]) >= 10]
            a[p, g + 8] = far[np.random.randint(len(far))]
    return np.exp2(a.ravel()).repeat(32)


def f64(x):
    return np.asarray(x).astype(np.float64)


def striped(idx):
    return np.tile(idx.reshape(-1, 16).T, (8, 1)).astype(np.uint16)


def unstriped(offs):
    return offs[:16].T.reshape(-1).astype(np.int64)


E2M1 = np.array([0.0, 0.5, 1.0, 1.5, 2.0, 3.0, 4.0, 6.0, -0.0, -0.5, -1.0, -1.5, -2.0, -3.0, -4.0, -6.0])


def pack_weight(w, fmt):
    k, n = w.shape
    w = f64(np.asarray(w, np.float32).astype(ml_dtypes.bfloat16)).reshape(k // 32, 32, n)
    amax = np.abs(w).max(1)
    if fmt == "e4m3":
        byte = np.frexp(amax)[1] - 1 + 127 - 7
    else:
        mant, ex = np.frexp(amax / 6.0)
        byte = np.where(mant > 0.5, ex, ex - 1) + 127
    byte = np.clip(np.where(amax > 0, byte, 1), 1, 254)
    scaled = (w * np.exp2(127.0 - byte)[:, None, :]).reshape(k, n).astype(np.float32)
    by_word = np.ascontiguousarray(scaled.reshape(k // 512, 128, 4, n).transpose(0, 1, 3, 2))
    if fmt == "e4m3":
        words = by_word.astype(ml_dtypes.float8_e4m3fn).view(np.uint8)
    else:
        c = by_word.astype(ml_dtypes.float4_e2m1fn).view(np.uint8) & 0xF
        words = (c[..., 0::2] | (c[..., 1::2] << 4)).reshape(k // 512, 128, 2 * n)
    return np.ascontiguousarray(words), np.ascontiguousarray(byte.astype(np.uint8).reshape(k // 512, 16, n))


def unpack_weight(words, scales, fmt):
    g, _, n = scales.shape
    words = np.ascontiguousarray(words).reshape(g, 128, n, -1)
    if fmt == "e4m3":
        vals = words.view(ml_dtypes.float8_e4m3fn).astype(np.float64)
    else:
        nib = np.empty((g, 128, n, 4), np.uint8)
        nib[..., 0::2] = words & 0xF
        nib[..., 1::2] = words >> 4
        vals = E2M1[nib]
    vals = vals * np.repeat(np.exp2(scales.astype(np.float64) - 127.0), 8, axis=1)[..., None]
    return vals.transpose(0, 1, 3, 2).reshape(g * 512, n)


def pack_table(v):
    words, scales = pack_weight(v, "e4m3")
    return np.concatenate([words.reshape(words.shape[0], -1), scales.reshape(scales.shape[0], -1)], axis=1)


def unpack_table(tab):
    g, t = tab.shape[0], tab.shape[1] // 528
    return unpack_weight(tab[:, :512 * t].reshape(g, 128, t, 4), tab[:, 512 * t:].reshape(g, 16, t), "e4m3")


G, K, M, T, S = 4, 512, 128, 4096, 512


def setup_inputs():
    n = np.random.standard_normal
    s = mx_kscale(K)[:, None]
    p_w4 = pack_weight(n((K, M)) / np.sqrt(K) / s, "e2m1")
    return {
        "tab": pack_table(n((K, T)) * s),
        "w4_words": p_w4[0],
        "w4_scales": p_w4[1],
        "dw": (0.3 * n((K, M)) / np.sqrt(K) / s).astype(np.float32),
        "offs": striped(np.concatenate([np.random.permutation(T)[:S] for _ in range(G)])),
    }


def reference(tab, w4_words, w4_scales, dw, offs):
    tab_ = unpack_table(tab)[:, unstriped(offs).reshape(G, S)].sum(1)
    w4_ = unpack_weight(w4_words, w4_scales, "e2m1")
    dw_ = mxq(f64(dw), 0, "e4m3")
    y = tab_.T @ w4_ + tab_.T @ dw_
    return y

@@ -1,0 +1,122 @@
+from contextlib import ExitStack
+
+import concourse.mybir as mybir
+
+G, K, M, T, S = 4, 512, 128, 4096, 512
+FLOPS = 2 * 2 * G * S * K * M
+
+F32 = mybir.dt.float32
+BF16 = mybir.dt.bfloat16
+I32 = mybir.dt.int32
+U32 = mybir.dt.uint32
+U16 = mybir.dt.uint16
+U8 = mybir.dt.uint8
+FP8X4 = mybir.dt.float8_e4m3fn_x4
+FP4X4 = mybir.dt.float4_e2m1fn_x4
+
+P = 128
+PACK = 4
+QUAD = 32
+BLOCKS = K // 32
+J_TILES = S // P
+LIST_COLS = S // 16
+HALF = G // 2
+
+
+def tile_list_tabbag_tm_sum_none_kernel(tc, tab, w4_words, w4_scales, dw, offs, out):
+    nc = tc.nc
+    with ExitStack() as ctx:
+        keep = ctx.enter_context(tc.tile_pool(name="keep", bufs=1))
+        psum = ctx.enter_context(tc.psum_pool(name="psum", bufs=1))
+
+        offsets = keep.tile([P, G * LIST_COLS], U16, name="offsets")
+        scale_win = keep.tile([P, T // 4], I32, name="scale_win", align_bytes=64)
+        word_win = keep.tile([P, T], I32, name="word_win", align_bytes=64)
+        w4_codes = keep.tile([P, M // 2], I32, name="w4_codes", align_bytes=64)
+        w4_plane = keep.tile([P, M // 4], I32, name="w4_plane", align_bytes=64)
+        dw_raw = keep.tile([P, PACK, M], F32, name="dw_raw", align_bytes=64)
+        dw_grouped = keep.tile([P, M, PACK], BF16, name="dw_grouped", align_bytes=64)
+        dw_codes = keep.tile([P, M], U32, name="dw_codes", align_bytes=64)
+        dw_plane = keep.tile([P, M], U8, name="dw_plane", align_bytes=64)
+        picked_scales = [keep.tile([P, HALF * S // 4], I32, name=f"picked_scales{h}", align_bytes=64) for h in range(2)]
+        planes = [keep.tile([P, HALF * S // 4], I32, name=f"plane{h}", align_bytes=64) for h in range(2)]
+        picked_words = [keep.tile([P, S], U32, name=f"picked_words{g}", align_bytes=64) for g in range(G)]
+        result = [keep.tile([P, M], F32, name=f"result{t}", align_bytes=64) for t in range(J_TILES)]
+        warm = keep.tile([P, 8], F32, name="warm")
+        warm_out = keep.tile([P, 8], BF16, name="warm_out")
+        acc = [psum.tile([P, M], F32, name=f"acc{t}") for t in range(J_TILES)]
+
+        last_quad = P - QUAD
+        nc.sync.dma_start(
+            scale_win[last_quad:, :],
+            tab[0, (K + BLOCKS - QUAD) * T :].rearrange("(p c) -> p c", p=QUAD).bitcast(I32),
+        )
+        nc.sync.dma_start(offsets[:], offs)
+        nc.sync.dma_start(word_win[:], tab[0, : K * T].rearrange("(p c) -> p c", p=P).bitcast(I32))
+        nc.vector.memset(scale_win[:last_quad, :], 0)
+        nc.vector.memset(w4_plane[:], 0)
+        nc.vector.memset(warm[:], 0.0)
+        for h in range(2):
+            nc.vector.memset(planes[h][:], 0)
+
+        nc.scalar.dma_start(w4_codes[:], w4_words[0].bitcast(I32))
+        for q in range(4):
+            nc.scalar.dma_start(w4_plane[QUAD * q : QUAD * q + 4, :], w4_scales[0, 4 * q : 4 * q + 4, :].bitcast(I32))
+        nc.scalar.copy(warm_out[:], warm[:])
+        nc.sync.dma_start(dw_raw[:], dw.rearrange("(p i) n -> p i n", i=PACK))
+
+        first_scale_row = P - BLOCKS
+        for h in range(2):
+            cols = slice(h * HALF * LIST_COLS, (h + 1) * HALF * LIST_COLS)
+            nc.vector.tensor_copy(picked_scales[h][:].bitcast(U8), scale_win[:].bitcast(U8).indirect(offsets[:, cols]))
+            for q in range(4):
+                rows = slice(first_scale_row + 4 * q, first_scale_row + 4 * q + 4)
+                nc.sync.dma_start(planes[h][QUAD * q : QUAD * q + 4, :], picked_scales[h][rows, :])
+
+        nc.scalar.copy(dw_grouped[:], dw_raw[:].rearrange("p i n -> p n i"))
+
+        def gather_words(g):
+            cols = slice(g * LIST_COLS, (g + 1) * LIST_COLS)
+            nc.vector.tensor_copy(picked_words[g][:], word_win[:].bitcast(U32).indirect(offsets[:, cols]))
+
+        def one_pass(g, t, rhs, rhs_scale, start, stop):
+            col0 = (g % HALF) * S + t * P
+            nc.tensor.matmul_mx(
+                out=acc[t][:],
+                lhsT=picked_words[g][:, t * P : (t + 1) * P].bitcast(FP8X4),
+                lhsT_scale=planes[g // HALF][:].bitcast(U8)[:, col0 : col0 + P],
+                rhs=rhs,
+                rhs_scale=rhs_scale,
+                start=start,
+                stop=stop,
+            )
+
+        def w4_pass(g, t):
+            one_pass(g, t, w4_codes[:].bitcast(FP4X4), w4_plane[:].bitcast(U8), g == 0, False)
+
+        def dw_pass(g, t):
+            one_pass(g, t, dw_codes[:].bitcast(FP8X4), dw_plane[:], False, g == G - 1)
+
+        gather_words(0)
+        for t in range(J_TILES):
+            w4_pass(0, t)
+        nc.vector.quantize_mx(
+            out=dw_codes[:].bitcast(FP8X4),
+            scales=dw_plane[:],
+            in_=dw_grouped[:].rearrange("p n i -> p (n i)"),
+        )
+        for t in range(J_TILES):
+            dw_pass(0, t)
+        for g in range(1, G):
+            gather_words(g)
+            for t in range(J_TILES):
+                w4_pass(g, t)
+                dw_pass(g, t)
+
+        for t in range(J_TILES):
+            if t % 2 == 0:
+                nc.scalar.copy(result[t][:], acc[t][:])
+                nc.scalar.dma_start(out[t * P : (t + 1) * P, :], result[t][:])
+            else:
+                nc.vector.tensor_copy(result[t][:], acc[t][:])
+                nc.sync.dma_start(out[t * P : (t + 1) * P, :], result[t][:])

@@ -34,13 +34,13 @@ def tile_list_tabbag_tm_sum_none_kernel(tc, tab, w4_words, w4_scales, dw, offs, 
         word_win = keep.tile([P, T], I32, name="word_win", align_bytes=64)
         w4_codes = keep.tile([P, M // 2], I32, name="w4_codes", align_bytes=64)
         w4_plane = keep.tile([P, M // 4], I32, name="w4_plane", align_bytes=64)
-        dw_raw = keep.tile([P, PACK, M], F32, name="dw_raw", align_bytes=64)
-        dw_grouped = keep.tile([P, M, PACK], BF16, name="dw_grouped", align_bytes=64)
+        dw_raw = keep.tile([P, PACK, M], F32, name="dw_raw", tag="shared_a", align_bytes=64)
+        dw_grouped = keep.tile([P, M, PACK], BF16, name="dw_grouped", tag="shared_b", align_bytes=64)
         dw_codes = keep.tile([P, M], U32, name="dw_codes", align_bytes=64)
         dw_plane = keep.tile([P, M], U8, name="dw_plane", align_bytes=64)
         picked_scales = [keep.tile([P, HALF * S // 4], I32, name=f"picked_scales{h}", align_bytes=64) for h in range(2)]
         planes = [keep.tile([P, HALF * S // 4], I32, name=f"plane{h}", align_bytes=64) for h in range(2)]
-        picked_words = [keep.tile([P, S], U32, name=f"picked_words{g}", align_bytes=64) for g in range(G)]
+        picked_words = {}
         result = [keep.tile([P, M], F32, name=f"result{t}", align_bytes=64) for t in range(J_TILES)]
         warm = keep.tile([P, 8], F32, name="warm")
         warm_out = keep.tile([P, 8], BF16, name="warm_out")
@@ -75,7 +75,8 @@ def tile_list_tabbag_tm_sum_none_kernel(tc, tab, w4_words, w4_scales, dw, offs, 
 
         nc.scalar.copy(dw_grouped[:], dw_raw[:].rearrange("p i n -> p n i"))
 
-        def gather_words(g):
+        def gather_words(g, tag):
+            picked_words[g] = keep.tile([P, S], U32, name=f"picked_words{g}", tag=tag, align_bytes=64)
             cols = slice(g * LIST_COLS, (g + 1) * LIST_COLS)
             nc.vector.tensor_copy(picked_words[g][:], word_win[:].bitcast(U32).indirect(offsets[:, cols]))
 
@@ -97,18 +98,20 @@ def tile_list_tabbag_tm_sum_none_kernel(tc, tab, w4_words, w4_scales, dw, offs, 
         def dw_pass(g, t):
             one_pass(g, t, dw_codes[:].bitcast(FP8X4), dw_plane[:], False, g == G - 1)
 
-        gather_words(0)
-        for t in range(J_TILES):
-            w4_pass(0, t)
+        for g in range(HALF):
+            gather_words(g, f"own{g}")
+            for t in range(J_TILES):
+                w4_pass(g, t)
         nc.vector.quantize_mx(
             out=dw_codes[:].bitcast(FP8X4),
             scales=dw_plane[:],
             in_=dw_grouped[:].rearrange("p n i -> p (n i)"),
         )
-        for t in range(J_TILES):
-            dw_pass(0, t)
-        for g in range(1, G):
-            gather_words(g)
+        for g in range(HALF):
+            for t in range(J_TILES):
+                dw_pass(g, t)
+        for g, tag in ((2, "shared_a"), (3, "shared_b")):
+            gather_words(g, tag)
             for t in range(J_TILES):
                 w4_pass(g, t)
                 dw_pass(g, t)

@@ -34,38 +34,33 @@ def tile_list_tabbag_tm_sum_none_kernel(tc, tab, w4_words, w4_scales, dw, offs, 
         word_win = keep.tile([P, T], I32, name="word_win", align_bytes=64)
         w4_codes = keep.tile([P, M // 2], I32, name="w4_codes", align_bytes=64)
         w4_plane = keep.tile([P, M // 4], I32, name="w4_plane", align_bytes=64)
-        dw_raw = keep.tile([P, PACK, M], F32, name="dw_raw", tag="shared_a", align_bytes=64)
-        dw_grouped = keep.tile([P, M, PACK], BF16, name="dw_grouped", tag="shared_b", align_bytes=64)
+        dw_raw = keep.tile([P, PACK, M], F32, name="dw_raw", align_bytes=64)
+        dw_grouped = keep.tile([P, M, PACK], BF16, name="dw_grouped", align_bytes=64)
         dw_codes = keep.tile([P, M], U32, name="dw_codes", align_bytes=64)
         dw_plane = keep.tile([P, M], U8, name="dw_plane", align_bytes=64)
         picked_scales = [keep.tile([P, HALF * S // 4], I32, name=f"picked_scales{h}", align_bytes=64) for h in range(2)]
         planes = [keep.tile([P, HALF * S // 4], I32, name=f"plane{h}", align_bytes=64) for h in range(2)]
-        picked_words = {}
+        picked_words = [keep.tile([P, S], U32, name=f"picked_words{g}", align_bytes=64) for g in range(G)]
         result = [keep.tile([P, M], F32, name=f"result{t}", align_bytes=64) for t in range(J_TILES)]
-        warm = keep.tile([P, 8], F32, name="warm")
-        warm_out = keep.tile([P, 8], BF16, name="warm_out")
         acc = [psum.tile([P, M], F32, name=f"acc{t}") for t in range(J_TILES)]
 
-        last_quad = P - QUAD
-        nc.sync.dma_start(
-            scale_win[last_quad:, :],
-            tab[0, (K + BLOCKS - QUAD) * T :].rearrange("(p c) -> p c", p=QUAD).bitcast(I32),
-        )
-        nc.sync.dma_start(offsets[:], offs)
-        nc.sync.dma_start(word_win[:], tab[0, : K * T].rearrange("(p c) -> p c", p=P).bitcast(I32))
-        nc.vector.memset(scale_win[:last_quad, :], 0)
+        first_scale_row = P - BLOCKS
         nc.vector.memset(w4_plane[:], 0)
-        nc.vector.memset(warm[:], 0.0)
+        nc.vector.memset(scale_win[:first_scale_row, :], 0)
         for h in range(2):
             nc.vector.memset(planes[h][:], 0)
 
-        nc.scalar.dma_start(w4_codes[:], w4_words[0].bitcast(I32))
+        nc.sync.dma_start(
+            scale_win[first_scale_row:, :],
+            tab[0, K * T :].rearrange("(p c) -> p c", p=BLOCKS).bitcast(I32),
+        )
+        nc.sync.dma_start(offsets[:], offs)
         for q in range(4):
             nc.scalar.dma_start(w4_plane[QUAD * q : QUAD * q + 4, :], w4_scales[0, 4 * q : 4 * q + 4, :].bitcast(I32))
-        nc.scalar.copy(warm_out[:], warm[:])
         nc.sync.dma_start(dw_raw[:], dw.rearrange("(p i) n -> p i n", i=PACK))
+        nc.sync.dma_start(word_win[:], tab[0, : K * T].rearrange("(p c) -> p c", p=P).bitcast(I32))
+        nc.sync.dma_start(w4_codes[:], w4_words[0].bitcast(I32))
 
-        first_scale_row = P - BLOCKS
         for h in range(2):
             cols = slice(h * HALF * LIST_COLS, (h + 1) * HALF * LIST_COLS)
             nc.vector.tensor_copy(picked_scales[h][:].bitcast(U8), scale_win[:].bitcast(U8).indirect(offsets[:, cols]))
@@ -74,47 +69,31 @@ def tile_list_tabbag_tm_sum_none_kernel(tc, tab, w4_words, w4_scales, dw, offs, 
                 nc.sync.dma_start(planes[h][QUAD * q : QUAD * q + 4, :], picked_scales[h][rows, :])
 
         nc.scalar.copy(dw_grouped[:], dw_raw[:].rearrange("p i n -> p n i"))
-
-        def gather_words(g, tag):
-            picked_words[g] = keep.tile([P, S], U32, name=f"picked_words{g}", tag=tag, align_bytes=64)
-            cols = slice(g * LIST_COLS, (g + 1) * LIST_COLS)
-            nc.vector.tensor_copy(picked_words[g][:], word_win[:].bitcast(U32).indirect(offsets[:, cols]))
-
-        def one_pass(g, t, rhs, rhs_scale, start, stop):
-            col0 = (g % HALF) * S + t * P
-            nc.tensor.matmul_mx(
-                out=acc[t][:],
-                lhsT=picked_words[g][:, t * P : (t + 1) * P].bitcast(FP8X4),
-                lhsT_scale=planes[g // HALF][:].bitcast(U8)[:, col0 : col0 + P],
-                rhs=rhs,
-                rhs_scale=rhs_scale,
-                start=start,
-                stop=stop,
-            )
-
-        def w4_pass(g, t):
-            one_pass(g, t, w4_codes[:].bitcast(FP4X4), w4_plane[:].bitcast(U8), g == 0, False)
-
-        def dw_pass(g, t):
-            one_pass(g, t, dw_codes[:].bitcast(FP8X4), dw_plane[:], False, g == G - 1)
-
-        for g in range(HALF):
-            gather_words(g, f"own{g}")
-            for t in range(J_TILES):
-                w4_pass(g, t)
         nc.vector.quantize_mx(
             out=dw_codes[:].bitcast(FP8X4),
             scales=dw_plane[:],
             in_=dw_grouped[:].rearrange("p n i -> p (n i)"),
         )
-        for g in range(HALF):
+
+        weights = (
+            (w4_codes[:].bitcast(FP4X4), w4_plane[:].bitcast(U8)),
+            (dw_codes[:].bitcast(FP8X4), dw_plane[:]),
+        )
+        for g in range(G):
+            cols = slice(g * LIST_COLS, (g + 1) * LIST_COLS)
+            nc.vector.tensor_copy(picked_words[g][:], word_win[:].bitcast(U32).indirect(offsets[:, cols]))
             for t in range(J_TILES):
-                dw_pass(g, t)
-        for g, tag in ((2, "shared_a"), (3, "shared_b")):
-            gather_words(g, tag)
-            for t in range(J_TILES):
-                w4_pass(g, t)
-                dw_pass(g, t)
+                col0 = (g % HALF) * S + t * P
+                for w, (rhs, rhs_scale) in enumerate(weights):
+                    nc.tensor.matmul_mx(
+                        out=acc[t][:],
+                        lhsT=picked_words[g][:, t * P : (t + 1) * P].bitcast(FP8X4),
+                        lhsT_scale=planes[g // HALF][:].bitcast(U8)[:, col0 : col0 + P],
+                        rhs=rhs,
+                        rhs_scale=rhs_scale,
+                        start=(g == 0 and w == 0),
+                        stop=(g == G - 1 and w == 1),
+                    )
 
         for t in range(J_TILES):
             if t % 2 == 0:

@@ -96,9 +96,6 @@ def tile_list_tabbag_tm_sum_none_kernel(tc, tab, w4_words, w4_scales, dw, offs, 
                     )
 
         for t in range(J_TILES):
-            if t % 2 == 0:
-                nc.scalar.copy(result[t][:], acc[t][:])
-                nc.scalar.dma_start(out[t * P : (t + 1) * P, :], result[t][:])
-            else:
-                nc.vector.tensor_copy(result[t][:], acc[t][:])
-                nc.sync.dma_start(out[t * P : (t + 1) * P, :], result[t][:])
+            nc.vector.tensor_copy(result[t][:], acc[t][:])
+            queue = nc.scalar if t % 2 == 0 else nc.sync
+            queue.dma_start(out[t * P : (t + 1) * P, :], result[t][:])

@@ -33,19 +33,17 @@ def tile_list_tabbag_tm_sum_none_kernel(tc, tab, w4_words, w4_scales, dw, offs, 
         scale_win = keep.tile([P, T // 4], I32, name="scale_win", align_bytes=64)
         word_win = keep.tile([P, T], I32, name="word_win", align_bytes=64)
         w4_codes = keep.tile([P, M // 2], I32, name="w4_codes", align_bytes=64)
-        w4_plane = keep.tile([P, M // 4], I32, name="w4_plane", align_bytes=64)
         dw_raw = keep.tile([P, PACK, M], F32, name="dw_raw", align_bytes=64)
         dw_grouped = keep.tile([P, M, PACK], BF16, name="dw_grouped", align_bytes=64)
         dw_codes = keep.tile([P, M], U32, name="dw_codes", align_bytes=64)
         dw_plane = keep.tile([P, M], U8, name="dw_plane", align_bytes=64)
-        picked_scales = [keep.tile([P, HALF * S // 4], I32, name=f"picked_scales{h}", align_bytes=64) for h in range(2)]
+        picked_scales = [keep.tile([P, HALF * S // 4], I32, name=f"picked_scales{h}", tag=f"picked{h}", align_bytes=64) for h in range(2)]
         planes = [keep.tile([P, HALF * S // 4], I32, name=f"plane{h}", align_bytes=64) for h in range(2)]
         picked_words = [keep.tile([P, S], U32, name=f"picked_words{g}", align_bytes=64) for g in range(G)]
         result = [keep.tile([P, M], F32, name=f"result{t}", align_bytes=64) for t in range(J_TILES)]
         acc = [psum.tile([P, M], F32, name=f"acc{t}") for t in range(J_TILES)]
 
         first_scale_row = P - BLOCKS
-        nc.vector.memset(w4_plane[:], 0)
         nc.vector.memset(scale_win[:first_scale_row, :], 0)
         for h in range(2):
             nc.vector.memset(planes[h][:], 0)
@@ -55,8 +53,6 @@ def tile_list_tabbag_tm_sum_none_kernel(tc, tab, w4_words, w4_scales, dw, offs, 
             tab[0, K * T :].rearrange("(p c) -> p c", p=BLOCKS).bitcast(I32),
         )
         nc.sync.dma_start(offsets[:], offs)
-        for q in range(4):
-            nc.scalar.dma_start(w4_plane[QUAD * q : QUAD * q + 4, :], w4_scales[0, 4 * q : 4 * q + 4, :].bitcast(I32))
         nc.sync.dma_start(dw_raw[:], dw.rearrange("(p i) n -> p i n", i=PACK))
         nc.sync.dma_start(word_win[:], tab[0, : K * T].rearrange("(p c) -> p c", p=P).bitcast(I32))
         nc.sync.dma_start(w4_codes[:], w4_words[0].bitcast(I32))
@@ -75,25 +71,44 @@ def tile_list_tabbag_tm_sum_none_kernel(tc, tab, w4_words, w4_scales, dw, offs, 
             in_=dw_grouped[:].rearrange("p n i -> p (n i)"),
         )
 
-        weights = (
-            (w4_codes[:].bitcast(FP4X4), w4_plane[:].bitcast(U8)),
-            (dw_codes[:].bitcast(FP8X4), dw_plane[:]),
-        )
-        for g in range(G):
+        w4_plane = keep.tile([P, M // 4], I32, name="w4_plane", tag="picked0", align_bytes=64)
+        for q in range(4):
+            nc.scalar.dma_start(w4_plane[QUAD * q : QUAD * q + 4, :], w4_scales[0, 4 * q : 4 * q + 4, :].bitcast(I32))
+
+        def gather_words(g):
             cols = slice(g * LIST_COLS, (g + 1) * LIST_COLS)
             nc.vector.tensor_copy(picked_words[g][:], word_win[:].bitcast(U32).indirect(offsets[:, cols]))
+
+        def one_pass(g, t, rhs, rhs_scale, start, stop):
+            col0 = (g % HALF) * S + t * P
+            nc.tensor.matmul_mx(
+                out=acc[t][:],
+                lhsT=picked_words[g][:, t * P : (t + 1) * P].bitcast(FP8X4),
+                lhsT_scale=planes[g // HALF][:].bitcast(U8)[:, col0 : col0 + P],
+                rhs=rhs,
+                rhs_scale=rhs_scale,
+                start=start,
+                stop=stop,
+            )
+
+        def w4_pass(g, t):
+            one_pass(g, t, w4_codes[:].bitcast(FP4X4), w4_plane[:].bitcast(U8), False, g == G - 1)
+
+        def dw_pass(g, t):
+            one_pass(g, t, dw_codes[:].bitcast(FP8X4), dw_plane[:], g == 0, False)
+
+        for g in range(HALF):
+            gather_words(g)
             for t in range(J_TILES):
-                col0 = (g % HALF) * S + t * P
-                for w, (rhs, rhs_scale) in enumerate(weights):
-                    nc.tensor.matmul_mx(
-                        out=acc[t][:],
-                        lhsT=picked_words[g][:, t * P : (t + 1) * P].bitcast(FP8X4),
-                        lhsT_scale=planes[g // HALF][:].bitcast(U8)[:, col0 : col0 + P],
-                        rhs=rhs,
-                        rhs_scale=rhs_scale,
-                        start=(g == 0 and w == 0),
-                        stop=(g == G - 1 and w == 1),
-                    )
+                dw_pass(g, t)
+        for g in range(HALF):
+            for t in range(J_TILES):
+                w4_pass(g, t)
+        for g in range(HALF, G):
+            gather_words(g)
+            for t in range(J_TILES):
+                dw_pass(g, t)
+                w4_pass(g, t)
 
         for t in range(J_TILES):
             nc.vector.tensor_copy(result[t][:], acc[t][:])

@@ -30,7 +30,7 @@ def tile_list_tabbag_tm_sum_none_kernel(tc, tab, w4_words, w4_scales, dw, offs, 
         psum = ctx.enter_context(tc.psum_pool(name="psum", bufs=1))
 
         offsets = keep.tile([P, G * LIST_COLS], U16, name="offsets")
-        scale_win = keep.tile([P, T // 4], I32, name="scale_win", align_bytes=64)
+        scale_win = keep.tile([P, T // 4], I32, name="scale_win", tag="scale_win", align_bytes=64)
         word_win = keep.tile([P, T], I32, name="word_win", align_bytes=64)
         w4_codes = keep.tile([P, M // 2], I32, name="w4_codes", align_bytes=64)
         dw_raw = keep.tile([P, PACK, M], F32, name="dw_raw", align_bytes=64)
@@ -57,12 +57,22 @@ def tile_list_tabbag_tm_sum_none_kernel(tc, tab, w4_words, w4_scales, dw, offs, 
         nc.sync.dma_start(word_win[:], tab[0, : K * T].rearrange("(p c) -> p c", p=P).bitcast(I32))
         nc.sync.dma_start(w4_codes[:], w4_words[0].bitcast(I32))
 
-        for h in range(2):
+        def gather_scales(h):
             cols = slice(h * HALF * LIST_COLS, (h + 1) * HALF * LIST_COLS)
             nc.vector.tensor_copy(picked_scales[h][:].bitcast(U8), scale_win[:].bitcast(U8).indirect(offsets[:, cols]))
+
+        def move_scales(h):
             for q in range(4):
                 rows = slice(first_scale_row + 4 * q, first_scale_row + 4 * q + 4)
                 nc.sync.dma_start(planes[h][QUAD * q : QUAD * q + 4, :], picked_scales[h][rows, :])
+
+        gather_scales(0)
+        move_scales(0)
+        gather_scales(1)
+        w4_plane = keep.tile([P, M // 4], I32, name="w4_plane", tag="scale_win", align_bytes=64)
+        for q in range(4):
+            nc.sync.dma_start(w4_plane[QUAD * q : QUAD * q + 4, :], w4_scales[0, 4 * q : 4 * q + 4, :].bitcast(I32))
+        move_scales(1)
 
         nc.scalar.copy(dw_grouped[:], dw_raw[:].rearrange("p i n -> p n i"))
         nc.vector.quantize_mx(
@@ -70,10 +80,6 @@ def tile_list_tabbag_tm_sum_none_kernel(tc, tab, w4_words, w4_scales, dw, offs, 
             scales=dw_plane[:],
             in_=dw_grouped[:].rearrange("p n i -> p (n i)"),
         )
-
-        w4_plane = keep.tile([P, M // 4], I32, name="w4_plane", tag="picked0", align_bytes=64)
-        for q in range(4):
-            nc.scalar.dma_start(w4_plane[QUAD * q : QUAD * q + 4, :], w4_scales[0, 4 * q : 4 * q + 4, :].bitcast(I32))
 
         def gather_words(g):
             cols = slice(g * LIST_COLS, (g + 1) * LIST_COLS)
@@ -97,14 +103,12 @@ def tile_list_tabbag_tm_sum_none_kernel(tc, tab, w4_words, w4_scales, dw, offs, 
         def dw_pass(g, t):
             one_pass(g, t, dw_codes[:].bitcast(FP8X4), dw_plane[:], g == 0, False)
 
-        for g in range(HALF):
-            gather_words(g)
-            for t in range(J_TILES):
-                dw_pass(g, t)
-        for g in range(HALF):
-            for t in range(J_TILES):
-                w4_pass(g, t)
-        for g in range(HALF, G):
+        gather_words(0)
+        for t in range(J_TILES):
+            dw_pass(0, t)
+        for t in range(J_TILES):
+            w4_pass(0, t)
+        for g in range(1, G):
             gather_words(g)
             for t in range(J_TILES):
                 dw_pass(g, t)

@@ -21,6 +21,7 @@ BLOCKS = K // 32
 J_TILES = S // P
 LIST_COLS = S // 16
 HALF = G // 2
+GATHER_TILES = (2,) * 8
 
 
 def tile_list_tabbag_tm_sum_none_kernel(tc, tab, w4_words, w4_scales, dw, offs, out):
@@ -33,13 +34,14 @@ def tile_list_tabbag_tm_sum_none_kernel(tc, tab, w4_words, w4_scales, dw, offs, 
         scale_win = keep.tile([P, T // 4], I32, name="scale_win", tag="scale_win", align_bytes=64)
         word_win = keep.tile([P, T], I32, name="word_win", align_bytes=64)
         w4_codes = keep.tile([P, M // 2], I32, name="w4_codes", align_bytes=64)
+        w4_plane = keep.tile([P, M // 4], I32, name="w4_plane", align_bytes=64)
         dw_raw = keep.tile([P, PACK, M], F32, name="dw_raw", align_bytes=64)
         dw_grouped = keep.tile([P, M, PACK], BF16, name="dw_grouped", align_bytes=64)
         dw_codes = keep.tile([P, M], U32, name="dw_codes", align_bytes=64)
         dw_plane = keep.tile([P, M], U8, name="dw_plane", align_bytes=64)
         picked_scales = [keep.tile([P, HALF * S // 4], I32, name=f"picked_scales{h}", tag=f"picked{h}", align_bytes=64) for h in range(2)]
         planes = [keep.tile([P, HALF * S // 4], I32, name=f"plane{h}", align_bytes=64) for h in range(2)]
-        picked_words = [keep.tile([P, S], U32, name=f"picked_words{g}", align_bytes=64) for g in range(G)]
+        picked_words = [keep.tile([P, n * P], U32, name=f"picked_words{c}", align_bytes=64) for c, n in enumerate(GATHER_TILES)]
         result = [keep.tile([P, M], F32, name=f"result{t}", align_bytes=64) for t in range(J_TILES)]
         acc = [psum.tile([P, M], F32, name=f"acc{t}") for t in range(J_TILES)]
 
@@ -53,6 +55,9 @@ def tile_list_tabbag_tm_sum_none_kernel(tc, tab, w4_words, w4_scales, dw, offs, 
             tab[0, K * T :].rearrange("(p c) -> p c", p=BLOCKS).bitcast(I32),
         )
         nc.sync.dma_start(offsets[:], offs)
+        for q in range(4):
+            rows = w4_scales[0, 4 * q : 4 * q + 4, :].bitcast(I32)
+            nc.scalar.dma_start(w4_plane[QUAD * q : QUAD * (q + 1), :], rows.unsqueeze(0).to_broadcast([QUAD // 4, 4, M // 4]))
         nc.sync.dma_start(dw_raw[:], dw.rearrange("(p i) n -> p i n", i=PACK))
         nc.sync.dma_start(word_win[:], tab[0, : K * T].rearrange("(p c) -> p c", p=P).bitcast(I32))
         nc.sync.dma_start(w4_codes[:], w4_words[0].bitcast(I32))
@@ -69,9 +74,6 @@ def tile_list_tabbag_tm_sum_none_kernel(tc, tab, w4_words, w4_scales, dw, offs, 
         gather_scales(0)
         move_scales(0)
         gather_scales(1)
-        w4_plane = keep.tile([P, M // 4], I32, name="w4_plane", tag="scale_win", align_bytes=64)
-        for q in range(4):
-            nc.sync.dma_start(w4_plane[QUAD * q : QUAD * q + 4, :], w4_scales[0, 4 * q : 4 * q + 4, :].bitcast(I32))
         move_scales(1)
 
         nc.scalar.copy(dw_grouped[:], dw_raw[:].rearrange("p i n -> p n i"))
@@ -81,15 +83,16 @@ def tile_list_tabbag_tm_sum_none_kernel(tc, tab, w4_words, w4_scales, dw, offs, 
             in_=dw_grouped[:].rearrange("p n i -> p (n i)"),
         )
 
-        def gather_words(g):
-            cols = slice(g * LIST_COLS, (g + 1) * LIST_COLS)
-            nc.vector.tensor_copy(picked_words[g][:], word_win[:].bitcast(U32).indirect(offsets[:, cols]))
+        def gather_words(c, first):
+            cols = slice(first * P // 16, (first + GATHER_TILES[c]) * P // 16)
+            nc.vector.tensor_copy(picked_words[c][:], word_win[:].bitcast(U32).indirect(offsets[:, cols]))
 
-        def one_pass(g, t, rhs, rhs_scale, start, stop):
+        def one_pass(c, i, slot, rhs, rhs_scale, start, stop):
+            g, t = divmod(slot, J_TILES)
             col0 = (g % HALF) * S + t * P
             nc.tensor.matmul_mx(
                 out=acc[t][:],
-                lhsT=picked_words[g][:, t * P : (t + 1) * P].bitcast(FP8X4),
+                lhsT=picked_words[c][:, i * P : (i + 1) * P].bitcast(FP8X4),
                 lhsT_scale=planes[g // HALF][:].bitcast(U8)[:, col0 : col0 + P],
                 rhs=rhs,
                 rhs_scale=rhs_scale,
@@ -97,22 +100,19 @@ def tile_list_tabbag_tm_sum_none_kernel(tc, tab, w4_words, w4_scales, dw, offs, 
                 stop=stop,
             )
 
-        def w4_pass(g, t):
-            one_pass(g, t, w4_codes[:].bitcast(FP4X4), w4_plane[:].bitcast(U8), False, g == G - 1)
+        def w4_pass(c, i, slot):
+            one_pass(c, i, slot, w4_codes[:].bitcast(FP4X4), w4_plane[:].bitcast(U8), False, slot // J_TILES == G - 1)
 
-        def dw_pass(g, t):
-            one_pass(g, t, dw_codes[:].bitcast(FP8X4), dw_plane[:], g == 0, False)
+        def dw_pass(c, i, slot):
+            one_pass(c, i, slot, dw_codes[:].bitcast(FP8X4), dw_plane[:], slot // J_TILES == 0, False)
 
-        gather_words(0)
-        for t in range(J_TILES):
-            dw_pass(0, t)
-        for t in range(J_TILES):
-            w4_pass(0, t)
-        for g in range(1, G):
-            gather_words(g)
-            for t in range(J_TILES):
-                dw_pass(g, t)
-                w4_pass(g, t)
+        first = 0
+        for c, n in enumerate(GATHER_TILES):
+            gather_words(c, first)
+            for i in range(n):
+                dw_pass(c, i, first + i)
+                w4_pass(c, i, first + i)
+            first += n
 
         for t in range(J_TILES):
             nc.vector.tensor_copy(result[t][:], acc[t][:])

@@ -21,7 +21,7 @@ BLOCKS = K // 32
 J_TILES = S // P
 LIST_COLS = S // 16
 HALF = G // 2
-GATHER_TILES = (2,) * 8
+GATHER_TILES = (2, 2, 4, 4, 2, 2)
 
 
 def tile_list_tabbag_tm_sum_none_kernel(tc, tab, w4_words, w4_scales, dw, offs, out):
@@ -55,12 +55,18 @@ def tile_list_tabbag_tm_sum_none_kernel(tc, tab, w4_words, w4_scales, dw, offs, 
             tab[0, K * T :].rearrange("(p c) -> p c", p=BLOCKS).bitcast(I32),
         )
         nc.sync.dma_start(offsets[:], offs)
-        for q in range(4):
-            rows = w4_scales[0, 4 * q : 4 * q + 4, :].bitcast(I32)
-            nc.scalar.dma_start(w4_plane[QUAD * q : QUAD * (q + 1), :], rows.unsqueeze(0).to_broadcast([QUAD // 4, 4, M // 4]))
         nc.sync.dma_start(dw_raw[:], dw.rearrange("(p i) n -> p i n", i=PACK))
+
+        def load_w4_scales(q):
+            rows = w4_scales[0, 4 * q : 4 * q + 4, :].bitcast(I32)
+            nc.sync.dma_start(w4_plane[QUAD * q : QUAD * (q + 1), :], rows.unsqueeze(0).to_broadcast([QUAD // 4, 4, M // 4]))
+
+        load_w4_scales(0)
+        load_w4_scales(1)
         nc.sync.dma_start(word_win[:], tab[0, : K * T].rearrange("(p c) -> p c", p=P).bitcast(I32))
         nc.sync.dma_start(w4_codes[:], w4_words[0].bitcast(I32))
+        load_w4_scales(2)
+        load_w4_scales(3)
 
         def gather_scales(h):
             cols = slice(h * HALF * LIST_COLS, (h + 1) * HALF * LIST_COLS)
@@ -115,6 +121,9 @@ def tile_list_tabbag_tm_sum_none_kernel(tc, tab, w4_words, w4_scales, dw, offs, 
             first += n
 
         for t in range(J_TILES):
-            nc.vector.tensor_copy(result[t][:], acc[t][:])
-            queue = nc.scalar if t % 2 == 0 else nc.sync
-            queue.dma_start(out[t * P : (t + 1) * P, :], result[t][:])
+            if t < GATHER_TILES[-1]:
+                nc.scalar.copy(result[t][:], acc[t][:])
+                nc.scalar.dma_start(out[t * P : (t + 1) * P, :], result[t][:])
+            else:
+                nc.vector.tensor_copy(result[t][:], acc[t][:])
+                nc.sync.dma_start(out[t * P : (t + 1) * P, :], result[t][:])

@@ -21,7 +21,7 @@ BLOCKS = K // 32
 J_TILES = S // P
 LIST_COLS = S // 16
 HALF = G // 2
-GATHER_TILES = (2, 2, 4, 4, 2, 2)
+GATHER_TILES = (5, 5, 4, 2)
 
 
 def tile_list_tabbag_tm_sum_none_kernel(tc, tab, w4_words, w4_scales, dw, offs, out):
@@ -115,7 +115,8 @@ def tile_list_tabbag_tm_sum_none_kernel(tc, tab, w4_words, w4_scales, dw, offs, 
         first = 0
         for c, n in enumerate(GATHER_TILES):
             gather_words(c, first)
-            for i in range(n):
+            closing_first = sorted(range(n), key=lambda i: (first + i) // J_TILES != G - 1)
+            for i in closing_first:
                 dw_pass(c, i, first + i)
                 w4_pass(c, i, first + i)
             first += n

@@ -21,7 +21,7 @@ BLOCKS = K // 32
 J_TILES = S // P
 LIST_COLS = S // 16
 HALF = G // 2
-GATHER_TILES = (5, 5, 4, 2)
+GATHER_TILES = (4, 4, 4, 2, 2)
 
 
 def tile_list_tabbag_tm_sum_none_kernel(tc, tab, w4_words, w4_scales, dw, offs, out):

@@ -46,6 +46,7 @@ def tile_list_tabbag_tm_sum_none_kernel(tc, tab, w4_words, w4_scales, dw, offs, 
         acc = [psum.tile([P, M], F32, name=f"acc{t}") for t in range(J_TILES)]
 
         first_scale_row = P - BLOCKS
+        nc.vector.memset(w4_plane[:], 0)
         nc.vector.memset(scale_win[:first_scale_row, :], 0)
         for h in range(2):
             nc.vector.memset(planes[h][:], 0)
@@ -59,7 +60,7 @@ def tile_list_tabbag_tm_sum_none_kernel(tc, tab, w4_words, w4_scales, dw, offs, 
 
         def load_w4_scales(q):
             rows = w4_scales[0, 4 * q : 4 * q + 4, :].bitcast(I32)
-            nc.sync.dma_start(w4_plane[QUAD * q : QUAD * (q + 1), :], rows.unsqueeze(0).to_broadcast([QUAD // 4, 4, M // 4]))
+            nc.sync.dma_start(w4_plane[QUAD * q : QUAD * q + 4, :], rows)
 
         load_w4_scales(0)
         load_w4_scales(1)

@@ -22,6 +22,7 @@ J_TILES = S // P
 LIST_COLS = S // 16
 HALF = G // 2
 GATHER_TILES = (4, 4, 4, 2, 2)
+CUT_MOVES = 3
 
 
 def tile_list_tabbag_tm_sum_none_kernel(tc, tab, w4_words, w4_scales, dw, offs, out):
@@ -73,10 +74,16 @@ def tile_list_tabbag_tm_sum_none_kernel(tc, tab, w4_words, w4_scales, dw, offs, 
             cols = slice(h * HALF * LIST_COLS, (h + 1) * HALF * LIST_COLS)
             nc.vector.tensor_copy(picked_scales[h][:].bitcast(U8), scale_win[:].bitcast(U8).indirect(offsets[:, cols]))
 
+        def move_rows(h, q, cols):
+            rows = slice(first_scale_row + 4 * q, first_scale_row + 4 * q + 4)
+            nc.sync.dma_start(planes[h][QUAD * q : QUAD * q + 4, cols], picked_scales[h][rows, cols])
+
         def move_scales(h):
+            cut = CUT_MOVES if h == 1 else 0
             for q in range(4):
-                rows = slice(first_scale_row + 4 * q, first_scale_row + 4 * q + 4)
-                nc.sync.dma_start(planes[h][QUAD * q : QUAD * q + 4, :], picked_scales[h][rows, :])
+                move_rows(h, q, slice(0, S // 4 if q < cut else HALF * S // 4))
+            for q in range(cut):
+                move_rows(h, q, slice(S // 4, HALF * S // 4))
 
         gather_scales(0)
         move_scales(0)
@@ -123,9 +130,6 @@ def tile_list_tabbag_tm_sum_none_kernel(tc, tab, w4_words, w4_scales, dw, offs, 
             first += n
 
         for t in range(J_TILES):
-            if t < GATHER_TILES[-1]:
-                nc.scalar.copy(result[t][:], acc[t][:])
-                nc.scalar.dma_start(out[t * P : (t + 1) * P, :], result[t][:])
-            else:
-                nc.vector.tensor_copy(result[t][:], acc[t][:])
-                nc.sync.dma_start(out[t * P : (t + 1) * P, :], result[t][:])
+            nc.vector.tensor_copy(result[t][:], acc[t][:])
+            queue = nc.sync if t % 2 else nc.scalar
+            queue.dma_start(out[t * P : (t + 1) * P, :], result[t][:])

from contextlib import ExitStack

import concourse.mybir as mybir

G, K, M, T, S = 4, 512, 128, 4096, 512
FLOPS = 2 * 2 * G * S * K * M

F32 = mybir.dt.float32
BF16 = mybir.dt.bfloat16
I32 = mybir.dt.int32
U32 = mybir.dt.uint32
U16 = mybir.dt.uint16
U8 = mybir.dt.uint8
FP8X4 = mybir.dt.float8_e4m3fn_x4
FP4X4 = mybir.dt.float4_e2m1fn_x4

P = 128
PACK = 4
QUAD = 32
BLOCKS = K // 32
J_TILES = S // P
LIST_COLS = S // 16
HALF = G // 2
GATHER_TILES = (4, 4, 4, 2, 2)
CUT_MOVES = 3


def tile_list_tabbag_tm_sum_none_kernel(tc, tab, w4_words, w4_scales, dw, offs, out):
    nc = tc.nc
    with ExitStack() as ctx:
        keep = ctx.enter_context(tc.tile_pool(name="keep", bufs=1))
        psum = ctx.enter_context(tc.psum_pool(name="psum", bufs=1))

        offsets = keep.tile([P, G * LIST_COLS], U16, name="offsets")
        scale_win = keep.tile([P, T // 4], I32, name="scale_win", tag="scale_win", align_bytes=64)
        word_win = keep.tile([P, T], I32, name="word_win", align_bytes=64)
        w4_codes = keep.tile([P, M // 2], I32, name="w4_codes", align_bytes=64)
        w4_plane = keep.tile([P, M // 4], I32, name="w4_plane", align_bytes=64)
        dw_raw = keep.tile([P, PACK, M], F32, name="dw_raw", align_bytes=64)
        dw_grouped = keep.tile([P, M, PACK], BF16, name="dw_grouped", align_bytes=64)
        dw_codes = keep.tile([P, M], U32, name="dw_codes", align_bytes=64)
        dw_plane = keep.tile([P, M], U8, name="dw_plane", align_bytes=64)
        picked_scales = [keep.tile([P, HALF * S // 4], I32, name=f"picked_scales{h}", tag=f"picked{h}", align_bytes=64) for h in range(2)]
        planes = [keep.tile([P, HALF * S // 4], I32, name=f"plane{h}", align_bytes=64) for h in range(2)]
        picked_words = [keep.tile([P, n * P], U32, name=f"picked_words{c}", align_bytes=64) for c, n in enumerate(GATHER_TILES)]
        result = [keep.tile([P, M], F32, name=f"result{t}", align_bytes=64) for t in range(J_TILES)]
        acc = [psum.tile([P, M], F32, name=f"acc{t}") for t in range(J_TILES)]

        first_scale_row = P - BLOCKS
        nc.vector.memset(w4_plane[:], 0)
        nc.vector.memset(scale_win[:first_scale_row, :], 0)
        for h in range(2):
            nc.vector.memset(planes[h][:], 0)

        nc.sync.dma_start(
            scale_win[first_scale_row:, :],
            tab[0, K * T :].rearrange("(p c) -> p c", p=BLOCKS).bitcast(I32),
        )
        nc.sync.dma_start(offsets[:], offs)
        nc.sync.dma_start(dw_raw[:], dw.rearrange("(p i) n -> p i n", i=PACK))

        def load_w4_scales(q):
            rows = w4_scales[0, 4 * q : 4 * q + 4, :].bitcast(I32)
            nc.sync.dma_start(w4_plane[QUAD * q : QUAD * q + 4, :], rows)

        load_w4_scales(0)
        load_w4_scales(1)
        nc.sync.dma_start(word_win[:], tab[0, : K * T].rearrange("(p c) -> p c", p=P).bitcast(I32))
        nc.sync.dma_start(w4_codes[:], w4_words[0].bitcast(I32))
        load_w4_scales(2)
        load_w4_scales(3)

        def gather_scales(h):
            cols = slice(h * HALF * LIST_COLS, (h + 1) * HALF * LIST_COLS)
            nc.vector.tensor_copy(picked_scales[h][:].bitcast(U8), scale_win[:].bitcast(U8).indirect(offsets[:, cols]))

        def move_rows(h, q, cols):
            rows = slice(first_scale_row + 4 * q, first_scale_row + 4 * q + 4)
            nc.sync.dma_start(planes[h][QUAD * q : QUAD * q + 4, cols], picked_scales[h][rows, cols])

        def move_scales(h):
            cut = CUT_MOVES if h == 1 else 0
            for q in range(4):
                move_rows(h, q, slice(0, S // 4 if q < cut else HALF * S // 4))
            for q in range(cut):
                move_rows(h, q, slice(S // 4, HALF * S // 4))

        gather_scales(0)
        move_scales(0)
        gather_scales(1)
        move_scales(1)

        nc.scalar.copy(dw_grouped[:], dw_raw[:].rearrange("p i n -> p n i"))
        nc.vector.quantize_mx(
            out=dw_codes[:].bitcast(FP8X4),
            scales=dw_plane[:],
            in_=dw_grouped[:].rearrange("p n i -> p (n i)"),
        )

        def gather_words(c, first):
            cols = slice(first * P // 16, (first + GATHER_TILES[c]) * P // 16)
            nc.vector.tensor_copy(picked_words[c][:], word_win[:].bitcast(U32).indirect(offsets[:, cols]))

        def one_pass(c, i, slot, rhs, rhs_scale, start, stop):
            g, t = divmod(slot, J_TILES)
            col0 = (g % HALF) * S + t * P
            nc.tensor.matmul_mx(
                out=acc[t][:],
                lhsT=picked_words[c][:, i * P : (i + 1) * P].bitcast(FP8X4),
                lhsT_scale=planes[g // HALF][:].bitcast(U8)[:, col0 : col0 + P],
                rhs=rhs,
                rhs_scale=rhs_scale,
                start=start,
                stop=stop,
            )

        def w4_pass(c, i, slot):
            one_pass(c, i, slot, w4_codes[:].bitcast(FP4X4), w4_plane[:].bitcast(U8), False, slot // J_TILES == G - 1)

        def dw_pass(c, i, slot):
            one_pass(c, i, slot, dw_codes[:].bitcast(FP8X4), dw_plane[:], slot // J_TILES == 0, False)

        first = 0
        for c, n in enumerate(GATHER_TILES):
            gather_words(c, first)
            closing_first = sorted(range(n), key=lambda i: (first + i) // J_TILES != G - 1)
            for i in closing_first:
                dw_pass(c, i, first + i)
                w4_pass(c, i, first + i)
            first += n

        for t in range(J_TILES):
            nc.vector.tensor_copy(result[t][:], acc[t][:])
            queue = nc.sync if t % 2 else nc.scalar
            queue.dma_start(out[t * P : (t + 1) * P, :], result[t][:])
